import numpy as np, ml_dtypes
CORES = [40,64,80,88,96,104,120,144]
N = 8
import mx_ref
BF = ml_dtypes.bfloat16
def gcols(t, e):
    v = np.concatenate([t.reshape(8, 16, -1, 4), np.zeros((8, 16, 1, 4), BF)], axis=2)
    return np.ascontiguousarray(np.stack([v[g][:, e[g]] for g in range(8)])).reshape(128, -1)
def tile(rs):
    return np.stack(rs, axis=2).reshape(128, -1).astype(BF)
def cut(t, i, w=512):
    return t[:, w * i:w * i + w]
def pick(q, e):
    c = np.concatenate([q[0].reshape(128, -1, 4), np.zeros((128, 1, 4), np.uint8)], axis=1); s = np.concatenate([q[1], np.ones((16, 1), np.uint8)], axis=1)
    return (np.ascontiguousarray(c[:, e].reshape(128, -1)), np.ascontiguousarray(s[:, e]))
def join(*qs):
    return (np.concatenate([q[0] for q in qs], axis=1), np.concatenate([q[1] for q in qs], axis=1))
def put(q, e, v):
    c, s = q[0].reshape(128, -1, 4).copy(), q[1].copy(); c[:, e] = v[0].reshape(128, -1, 4); s[:, e] = v[1]
    return (c.reshape(128, -1), s)
def pk(c, s):
    return (np.ascontiguousarray(c), mx_ref.live(s))
def emit(q):
    return q[0], q[1]
def packed(v, rng):
    q = [mx_ref.quantize(np.ascontiguousarray(v[r])) for r in range(N)]
    return np.stack([a for a, b in q]), np.stack([mx_ref.plane(b, rng) for a, b in q])
def values_of_codes():
    e, c = np.zeros((128, 128, 4), np.float32), np.zeros((128, 2, 4), np.uint8)
    e[np.arange(128), np.arange(128), 0] = 1
    c[:127, :, 0] = np.arange(256).reshape(2, 128).T[:127]
    return mx_ref.matmul(mx_ref.quantize(e.reshape(128, 512).astype(BF)), (c.reshape(128, 8), np.full((16, 2), 127, np.uint8))).T.reshape(-1).astype(np.float64)
CODE_VALUE, SCALE_VALUE = values_of_codes(), 2.0 ** (np.arange(256) - 127.0)
def decode(q):
    return (CODE_VALUE[q[0]].reshape(16, 8, -1, 4) * SCALE_VALUE[q[1]][:, None, :, None] + 0.0).reshape(128, -1).astype(np.float32)
def f(rng, *shape):
    return mx_ref.flush((rng.standard_normal(shape, dtype=np.float32) * np.exp2(rng.integers(-2, 3, shape[:-1] + (1,)))).astype(BF))
def wide(rng, *shape, cols=0):
    v = rng.standard_normal(shape, dtype=np.float32) * np.exp2(rng.integers(-12, 13, shape)).astype(np.float32)
    if cols: v *= np.repeat(np.exp2(rng.integers(-cols, cols + 1, shape[:-2] + (1, shape[-1] // 4))) * (rng.random(shape[:-2] + (1, shape[-1] // 4)) > 0.0625), 4, axis=-1).astype(np.float32)
    return mx_ref.flush(v.astype(BF))
C, H, E, R = 288, 96, 384, 3
def big(v):
    v = v.astype(np.float32)
    v[np.abs(v) < np.float32(2.0 ** -16)] = 0
    return v.astype(BF)
def numbers_of(rng):
    return {"x": big(f(rng, N, 128, 4 * C)), "u": np.array(f(rng, N, 128, 512)), "v": np.array(f(rng, N, 128, 512))}
def layers(rng):
    return big(f(rng, N, 128, 2048)).reshape(N, 8, 16, 4, 8, 16, 4)
def weights(rng, w):
    c, p = packed(np.ascontiguousarray(w).reshape(N, 128, 2048), rng)
    return {"wc": c, "ws": p}
def setup_inputs(rng):
    return {**numbers_of(rng), **weights(rng, layers(rng))}
def setup_inputs_ties(rng):
    d = numbers_of(rng)
    e = rng.permutation(N)
    x = d["x"].reshape(N, 8, 16, C, 4)
    for r in range(N):
        k = rng.permutation(C) % 3
        if r == e[0]: k = np.zeros(C, int)
        elif r in e[2::2]: k = rng.permutation(3)[np.arange(C) % 3]
        a = x[r][:, :8, :3].copy()
        a[:, :, 2] = 0
        x[r][:, :8] = a[:, :, k]
    x[e[1]] = 0
    u = d["u"].reshape(N, 8, 16, 128, 4)
    u[:, :, 8:, ::16] = 0
    u[:, :, 8:, 1::16] = 0
    w = layers(rng)
    w[:, :, :, :, :, :8] = 0
    return {"x": x.reshape(N, 128, 4 * C), "u": u.reshape(N, 128, 512), "v": d["v"], **weights(rng, w)}
def setup_inputs_near(rng):
    d = numbers_of(rng)
    x = d["x"].reshape(N, 8, 16, C, 4)
    u = d["u"].reshape(N, 128, 128, 4)
    o = rng.permutation(N) % 4
    x[:, :, :8] = 0
    u[:, :, ::16] = 0
    u[:, :, 1::16] = 0
    for r in range(N):
        s = rng.integers(-1, 2, (8, 2, C)).astype(np.float32)
        if o[r] % 2 == 1: s = s[:, :, np.arange(C) // 16]
        if o[r] < 2: s = s * np.float32(2.0 ** -29)
        for g in rng.permutation(8)[:4]: s[g, :, rng.integers(C)] = 2.0 ** 29 * rng.choice([-1.0, 1.0], 2)
        x[r, :, :2, :, 0] = s.astype(BF)
        for h in range(0, 128, 16):
            u[r, h, h, 0] = 2.0 ** -30 if o[r] < 2 else 1.0
            u[r, h + 1, h + 1, 0] = 2.0 ** -30 if o[r] < 2 else 1.0
    w = layers(rng)
    w[:, :, :8] = 0
    w[:, :, :, :, :, :8] = 0
    return {"x": x.reshape(N, 128, 4 * C), "u": u.reshape(N, 128, 512), "v": d["v"], **weights(rng, w)}
def setup_inputs_late(rng):
    d = numbers_of(rng)
    x = d["x"].reshape(N, 8, 16, C, 4)
    c = (rng.permutation(N) % 2 * 2.0 - 1.0).astype(np.float32).astype(BF)
    x[:, :, 0] = c[:, None, None, None]
    u = d["u"].reshape(N, 128, 128, 4)
    u[:, :, ::16] = 0
    u[:, :, 1::16] = 0
    for h in range(0, 128, 16):
        u[:, h, h, 0] = 1
        u[:, h, h + 1, 1] = 1
    return {"x": x.reshape(N, 128, 4 * C), "u": u.reshape(N, 128, 512), "v": d["v"], **weights(rng, layers(rng))}
def setup_inputs_huge(rng):
    d = numbers_of(rng)
    h = rng.permutation(8)
    x = -0.95 - 0.05 * rng.random((N, 8, 16, C, 4))
    x[:, h[4:]] = (0.75 + 0.1 * rng.random((N, 4, 16, C, 4))) * rng.choice([-1.0, 1.0], (N, 4, 1, C, 1))
    u = d["u"].reshape(N, 128, 128, 4)
    u[:, :, ::16] = 0
    u[:, :, 1::16] = 0
    for r in range(N):
        for g in range(8):
            for b in range(2):
                a = 16 * int(rng.choice(h[4:]))
                u[r, a:a + 16, 16 * g + b] = (2.0 ** 30 * (1 - 0.1 * rng.random((16, 4))) * rng.choice([-1.0, 1.0])).astype(np.float32).astype(BF)
    w = np.zeros((N, 128, 4, 128, 4), np.float32)
    i = np.arange(128)
    for b in range(4): w[:, i, b, i, b] = -1
    return {"x": (2.0 ** 30 * x).astype(np.float32).reshape(N, 128, 4 * C).astype(BF), "u": u.reshape(N, 128, 512), "v": d["v"], **weights(rng, w.astype(BF))}
def setup_inputs_spread(rng):
    d = setup_inputs(rng)
    d["x"] = big(wide(rng, N, 128, 4 * C, cols=6))
    return d
def check_inputs(d):
    b = []
    for k in ("x", "u", "v"):
        a = np.abs(d[k].astype(np.float32))
        if not (np.isfinite(a).all() and ((a == 0) | (a >= 2.0 ** -30) & (a <= 2.0 ** 30)).all()): b.append("a value of " + k)
    none, least, most = [emit(mx_ref.quantize(np.full((128, 16), k, np.float32).astype(BF)))[1][0, 0] for k in (0.0, 2.0 ** -30, 2.0 ** 30)]
    for r in range(N):
        if ((d["wc"][r] == 0x7F) | (d["wc"][r] == 0xFF)).any(): b.append("wc: a code that is no number")
        s = mx_ref.live(d["ws"][r])
        if ((s != none) & ((s < least) | (s > most))).any(): b.append("ws: a scale out of range")
    return b
def reference(x, u, v, wc, ws):
    qu = [mx_ref.quantize(u[r]) for r in range(N)]
    lay = [pk(wc[r], ws[r]) for r in range(N)]
    now = [x[r] for r in range(N)]
    level = np.zeros((N, 8, E), np.int64)
    for t in range(R):
        d = 2 ** t
        q = [mx_ref.quantize(now[r]) for r in range(N)]
        halo = [pick(q[r], np.arange(H)) for r in range(N)]
        came = decode(join(*halo)).astype(BF)
        made = []
        for r in range(N):
            e = (r + 1) % N
            s = mx_ref.matmul(qu[r], join(q[r], halo[e]))
            if t == 0: word = 2 * (s[::16] > 0) + (s[1::16] > 0)
            else: word = 2 * level[r] + (s[::16] > 0)
            key = 1024 * word
            key[:, :E - d] += 1 + word[:, d:]
            o = np.argsort(key, axis=1, kind="stable")
            for g in range(8): level[r, g] = np.searchsorted(key[g, o[g]], key[g])
            n, m = np.zeros((8, E), np.int64), np.zeros((8, E), np.int64)
            np.put_along_axis(n, o, np.concatenate([o[:, :1], o[:, :-1]], axis=1), axis=1)
            np.put_along_axis(m, o, np.concatenate([o[:, 1:], o[:, -1:]], axis=1), axis=1)
            a = np.concatenate([now[r], cut(came, e, 4 * H)], axis=1)
            most = np.maximum(gcols(a, n[:, :C]).astype(np.float32), gcols(a, m[:, :C]).astype(np.float32))
            z = mx_ref.quantize(((now[r].astype(np.float32) + most) * np.float32(0.5)).astype(BF))
            made.append(tile([mx_ref.matmul(pick(lay[r], np.arange(128 * b, 128 * b + 128)), z) * np.float32(0.03125) + now[r][:, b::4].astype(np.float32) for b in range(4)]))
        now = made
    y, lv = np.zeros((N, 128, C), np.float32), np.zeros((N, 8, E), np.float32)
    oc, osc = np.zeros((N, 128, 4 * C), np.uint8), np.zeros((N, 16, C), np.uint8)
    for r in range(N):
        q = mx_ref.quantize(now[r])
        y[r] = mx_ref.matmul(mx_ref.quantize(v[r]), q)
        lv[r] = level[r]
        oc[r], osc[r] = emit(q)
    return {"y": y, "lv": lv, "oc": oc, "osc": osc}

from concourse.mybir import dt, AluOpType as Alu, ActivationFunctionType as Act

C, H, E, R = 288, 96, 384, 3
NC = E // 16
NV = 8
PRE = 256
NP = PRE // 16
BL = 16 * NV + 2
SETS = ((0, 8, 128), (8, 12, 192), (12, 16, 256), (16, 20, 320), (20, 24, 384))
CW = 320
LATE = ((16, 17, 18, 19), (19,))
CENTER = 7130000
MULT = (5.0, 44.0, 771.0)
UNIT = (48.0, 24.0, 24.0)
HOLD = 2.0 ** 25

X4, U8, BF, F32, I32, U16, F16 = "float8_e4m3fn_x4", "uint8", "bfloat16", "float32", "int32", "uint16", "float16"
SCRATCH = {}
for _n, _w, _d in [
    ("xin", 4 * C, BF), ("uin", 512, BF), ("vin", 512, BF), ("wq", 512, X4), ("wp", 512, U8),
    ("uq", 128, X4), ("up", 128, U8), ("ua", 256, X4), ("uap", 256, U8), ("vq", 128, X4), ("vp", 128, U8),
    ("ones", 512, BF), ("ident", 128, BF), ("et", 2048, BF), ("eq", 512, X4), ("ep", 512, U8),
    ("za", 512, BF), ("zb", 768, BF), ("zqa", 128, X4), ("zpa", 128, U8), ("zqb", 192, X4), ("zpb", 192, U8),
    ("gn", 4 * C, BF), ("gm", 4 * C, BF), ("x32", 4 * C, BF), ("xt", 4 * C, BF), ("vh", 4 * E, BF),
    ("sa", E, BF), ("sb", E, BF), ("w16", E, BF), ("wf", E, F32), ("wm16", E, BF), ("wmf", E, F32),
    ("k16", E, BF), ("kf", E, F32), ("ka", E, F32), ("ka16", E, F16), ("ksc16", E, BF), ("ksc", E, F32),
    ("thx", NC, F32), ("th", NC, F32), ("bits", NV * BL, BF), ("rst", NV * BL, BF), ("cnt", NV * BL, F16),
    ("tl1", 768, BF), ("tl2", 1024, BF), ("tl3", 1280, BF), ("tl4", 1536, BF), ("zero", 768, BF), ("bu", 512, BF), ("bt", 512, BF),
    ("bq", 128, X4), ("bp", 128, U8), ("cnu", 4 * CW, F16), ("ext", E, F32), ("m16", CW, BF), ("pc0", NC, F32), ("pc1", NC, F32),
    ("acc", NC, F32), ("acc1", NC, F32), ("acc2", NC, F32),
    ("pos", NC, U16), ("nmo", 36, U16), ("ordw", E, F32), ("nm", 2 * C, F16), ("nms", 2 * C, F16), ("off", 2 * C // 4, U16),
    ("osc0", E, F32), ("oo", NC, U16), ("ks", E, F32), ("kd", E, F32), ("lvs", E, F32), ("pp", E, F32), ("ysb", C, F32),
    ("t1", 16, I32), ("t2", 16, I32), ("t3", 16, I32), ("t4", 16, I32), ("t5", 16, I32), ("k1", E, F32),
    ("st", E, F32), ("st16", E, F16), ("mk", E, BF), ("m4", E, BF), ("ma", 48, BF), ("mb", 48, BF),
    ("cci", NC, I32), ("ccj", NC, I32), ("cc", NC, F32), ("cc0", NC, F32), ("uoi", 16, I32), ("uo", 16, U16),
    ("pi", 4, I32), ("pf", 6, F32),
]:
    SCRATCH[_n] = ("sbuf", [128, _w], _d)
for _t in range(R + 1):
    SCRATCH["q%d" % _t] = ("sbuf", [128, E], X4)
    SCRATCH["s%d" % _t] = ("sbuf", [128, E], U8)
    SCRATCH["tq%d" % (_t + 1)] = ("sbuf", [128, CW], X4)
    SCRATCH["tp%d" % (_t + 1)] = ("sbuf", [128, CW], U8)
for _t in range(R):
    SCRATCH["rc%d" % _t] = ("sbuf", [128, H], X4)
    SCRATCH["rs%d" % _t] = ("sbuf", [128, H], U8)
for _t in range(8):
    SCRATCH["ps%d" % _t] = ("psum", [128, 512], F32)

SEMAPHORES = ["cv", "ca", "cp", "cg", "sent", "lxa", "lxb", "lu", "lvv", "lw", "out"] + \
    ["arr%d" % _t for _t in range(R)] + ["rl%d" % _t for _t in range(R)]


def bitmask(engines):
    m = 0
    for e in engines:
        m |= 1 << e
    return m


def helpers(topo, src, dst):
    if topo.may_write(src, dst):
        return []
    c = [k for k in topo.cores_of(src) if k != src and topo.may_write(k, dst)]
    c.sort(key=lambda k: topo.die(k) != topo.die(src))
    return c[:2]


def hand_on(g, core, T, topo, dst, which, came):
    rid, pid = topo.addr(dst, core)
    n = len(topo.engines(core, dst))
    for t in range(R):
        g.wait_ge(T.sem["rl%d" % t], came)
        if which == 0:
            o, i = T["q%d" % t][:, C:E].bitcast(dt.uint8), T["rc%d" % t][:, :].bitcast(dt.uint8)
        else:
            o, i = T["s%d" % t][:, C:E], T["rs%d" % t][:, :]
        g.remote_dma(o, i, T.sem["arr%d" % t], T.sem.sent, pid, rid, topo.mask(core, dst))
    g.wait_ge(T.sem.sent, n * R)


def rank_program(g, core, T, topo):
    N = len(T.cores)
    rank = T.rank_of(core)
    if rank is None:
        for r in range(N):
            src, dst = T.cores[r], T.cores[(r - 1) % N]
            hs = helpers(topo, src, dst)
            if core in hs:
                hand_on(g, core, T, topo, dst, hs.index(core), len(topo.engines(src, core)) // 2)
        return

    V, A, P = g.vector, g.scalar, g.tensor
    queue = {"v": V, "a": A, "p": P, "g": g, "s": g.sync}
    total, seen, wrote, read = {}, {k: {} for k in queue}, {}, {}

    def need(e, sem, val):
        if seen[e].get(sem, 0) < val:
            queue[e].wait_ge(T.sem[sem], val)
            seen[e][sem] = val

    def op(e, call, r=(), w=(), sem=None):
        want = {}
        for tag in tuple(r) + tuple(w):
            if tag in wrote:
                s, v = wrote[tag]
                want[s] = max(want.get(s, 0), v)
        for tag in w:
            for s, v in read.get(tag, {}).items():
                want[s] = max(want.get(s, 0), v)
        for s, v in want.items():
            need(e, s, v)
        s, inc = (sem, 16) if sem else ("c" + e, 1)
        call().then_inc(T.sem[s], inc)
        total[s] = total.get(s, 0) + inc
        for tag in r:
            read.setdefault(tag, {})[s] = total[s]
        for tag in w:
            wrote[tag] = (s, total[s])
            read[tag] = {}

    def ts(out, in0, s1, s2, o0, o1=None, r=(), w=()):
        if o1 is None:
            op("v", lambda: V.tensor_scalar(out, in0, s1, None, o0), r, w)
        else:
            op("v", lambda: V.tensor_scalar(out, in0, s1, s2, o0, o1), r, w)

    def tt(out, a, b, o, r=(), w=()):
        op("v", lambda: V.tensor_tensor(out, a, b, o), r, w)

    def cp(out, a, r=(), w=()):
        op("v", lambda: V.tensor_copy(out, a), r, w)

    def scan(out, a, b, init, o0, o1, r=(), w=()):
        op("v", lambda: V.tensor_tensor_scan(out, a, b, init, o0, o1), r, w)

    def fill(out, c, w):
        op("v", lambda: V.memset(out, c), (), w)

    def quant(q, s, a, r, w):
        op("v", lambda: V.quantize_mx(q, s, a), r, w)

    def act(out, a, f, r=(), w=(), **kw):
        op("a", lambda: A.activation(out, a, f, **kw), r, w)

    def mm(bank, n, lq, lp, rq, rp, r):
        op("p", lambda: P.matmul_mx(T["ps%d" % bank][:, 0:n], lq, lp, rq, rp, True, True), r, ["ps%d" % bank])

    def iota(out, pat, base, cm, w, small=False):
        if small:
            op("g", lambda: g.iota(out, pat, base, cm, allow_small_or_imprecise_dtypes=True), (), w)
        else:
            op("g", lambda: g.iota(out, pat, base, cm), (), w)

    def tags(name, lo, hi):
        return ["%s%d" % (name, c) for c in range(lo, hi)]

    def repeat(buf, tag, n, end, step=None):
        while n < end:
            m = min(n, end - n)
            if step:
                act(buf[:, n:n + m], buf[:, 0:m], Act.Identity, [tag], [tag], bias=n * step)
            else:
                act(buf[:, n:n + m], buf[:, 0:m], Act.Copy, [tag], [tag])
            n += m
            yield

    before, nxt = T.cores[(rank - 1) % N], T.cores[(rank + 1) % N]
    hs = helpers(topo, core, before)
    senders = helpers(topo, nxt, core) or [nxt, nxt]
    for t in range(R):
        total["arr%d" % t] = sum(len(topo.engines(k, core)) for k in senders)
        wrote["halo%d" % t] = ("arr%d" % t, total["arr%d" % t])
    total["sent"] = 0

    def send(t):
        s, v = wrote["qa%d" % t]
        need("g", s, v)
        parts = [(T["q%d" % t][:, 0:H].bitcast(dt.uint8), T["q%d" % t][:, C:E].bitcast(dt.uint8), T["rc%d" % t][:, :].bitcast(dt.uint8)),
                 (T["s%d" % t][:, 0:H], T["s%d" % t][:, C:E], T["rs%d" % t][:, :])]
        for k in range(2):
            src, far, near = parts[k]
            if hs:
                en = topo.engines(core, hs[k])
                en = en[k * (len(en) // 2):(k + 1) * (len(en) // 2)]
                rid, pid = topo.addr(hs[k], core)
                g.remote_dma(near, src, T.sem["rl%d" % t], T.sem.sent, pid, rid, bitmask(en))
            else:
                en = topo.engines(core, before)
                rid, pid = topo.addr(before, core)
                g.remote_dma(far, src, T.sem["arr%d" % t], T.sem.sent, pid, rid, bitmask(en))
            total["sent"] += len(en)

    op("s", lambda: g.sync.dma_start(T.xin[:, 0:512], T.x[:, 0:512]), (), ["xa"], "lxa")
    op("a", lambda: A.dma_start(T.xin[:, 512:4 * C], T.x[:, 512:4 * C]), (), ["xb"], "lxb")
    op("s", lambda: g.sync.dma_start(T.uin[:, :], T.u[:, :]), (), ["uin"], "lu")
    op("s", lambda: g.sync.dma_start(T.wq[:, :].bitcast(dt.uint8), T.wc[:, :]), (), ["W0"], "lw")
    op("s", lambda: g.sync.dma_start(T.wp[:, :], T.ws[:, :]), (), ["W"], "lw")
    op("s", lambda: g.sync.dma_start(T.vin[:, :], T.v[:, :]), (), ["vin"], "lvv")

    iota(T.t1[:, :], [[1, 16]], 128, -1, ["t1"])
    iota(T.t2[:, :], [[4, 16]], 131, -1, ["t2"])
    iota(T.uoi[:, :], [[1, 2], [16, 8]], 0, 0, ["uoi"])
    iota(T.cci[:, :], [[16, NC]], 143, -1, ["cci"])
    iota(T.pi[:, 0:1], [[0, 1]], 0, 1, ["pi0"])
    iota(T.rst[:, 0:BL], [[4, BL]], 0, 0, ["rst"], True)
    fill(T.ones[:, :], 1.0, ["ones"])
    op("g", lambda: g.affine_select(T.ident[:, :], T.ones[:, 0:128], [[1, 128]], Alu.is_equal, 0.0, 0, -1), ["ones"], ["ident"])
    fill(T.za[:, 4 * H:512], 0.0, ["zapad"])
    ts(T.t3[:, :], T.t1[:, :], 15, None, Alu.bitwise_and, r=["t1"], w=["t3"])
    ts(T.t4[:, :], T.t1[:, :], 4, None, Alu.arith_shift_right, r=["t1"], w=["t4"])
    ts(T.t5[:, :], T.t2[:, :], 2, 3, Alu.arith_shift_right, Alu.bitwise_and, r=["t2"], w=["t5"])
    ts(T.ma[:, 0:16], T.t3[:, :], 1.0, HOLD, Alu.is_equal, Alu.mult, r=["t3"], w=["ma0"])
    ts(T.mb[:, 0:16], T.t3[:, :], 0.0, None, Alu.not_equal, r=["t3"], w=["mb0"])
    ts(T.st[:, 0:16], T.t4[:, :], 0.5 - CENTER, None, Alu.add, r=["t4"], w=["st"])
    ts(T.ma[:, 16:32], T.t5[:, :], 1.0, 512.0, Alu.is_equal, Alu.mult, r=["t5"], w=["ma1"])
    ts(T.mb[:, 16:32], T.t5[:, :], 0.0, -2048.0, Alu.is_equal, Alu.mult, r=["t5"], w=["mb1"])
    ts(T.ma[:, 32:48], T.t3[:, :], 1.0, 512.0, Alu.is_equal, Alu.mult, r=["t3"], w=["ma2"])
    ts(T.mb[:, 32:48], T.t3[:, :], 0.0, -2048.0, Alu.is_equal, Alu.mult, r=["t3"], w=["mb2"])
    tt(T.mk[:, 0:16], T.ma[:, 0:16], T.mb[:, 0:16], Alu.max, ["ma0", "mb0"], ["mk"])
    tt(T.m4[:, 0:16], T.ma[:, 16:32], T.mb[:, 16:32], Alu.add, ["ma1", "mb1"], ["m4"])
    tt(T.m16[:, 0:16], T.ma[:, 32:48], T.mb[:, 32:48], Alu.add, ["ma2", "mb2"], ["m16"])
    cp(T.uo[:, :], T.uoi[:, :], ["uoi"], ["uo"])
    ts(T.pf[:, 0:1], T.t3[:, 0:1], 1.0, 1.0 / HOLD, Alu.is_equal, Alu.max, r=["t3"], w=["pf0"])
    ts(T.ccj[:, :], T.cci[:, :], 4, None, Alu.arith_shift_right, r=["cci"], w=["ccj"])
    ts(T.pi[:, 1:2], T.pi[:, 0:1], 3, None, Alu.bitwise_and, r=["pi0"], w=["pi1"])
    ts(T.pi[:, 2:3], T.pi[:, 0:1], 2, 3, Alu.arith_shift_right, Alu.bitwise_and, r=["pi0"], w=["pi2"])
    ts(T.pf[:, 4:5], T.t3[:, 0:1], 1.0, 512.0, Alu.not_equal, Alu.mult, r=["t3"], w=["pf4"])
    ts(T.cc[:, :], T.ccj[:, :], float(-CENTER), None, Alu.add, r=["ccj"], w=["cc"])
    cp(T.cc0[:, :], T.ccj[:, :], ["ccj"], ["cc0"])
    ts(T.pf[:, 1:2], T.pi[:, 1:2], -4.0, None, Alu.add, r=["pi1"], w=["pf1"])
    ts(T.pf[:, 2:3], T.pi[:, 2:3], 3.0, -2048.0, Alu.is_lt, Alu.mult, r=["pi2"], w=["pf2"])
    fill(T.bits[:, 0:NV * BL:BL], 0.0, ["bz0"])
    fill(T.bits[:, 1:NV * BL:BL], 0.0, ["bz1"])
    tt(T.pf[:, 3:4], T.pf[:, 1:2], T.pf[:, 2:3], Alu.add, ["pf1", "pf2"], ["pf3"])
    for _ in zip(repeat(T.mk, "mk", 16, E), repeat(T.st, "st", 16, E, 1 / 16)):
        pass

    quant(T.q0[:, 0:128], T.s0[:, 0:128], T.xin[:, 0:512], ["xa"], ["qa0"])
    send(0)
    op("g", lambda: g.affine_select(T.bu[:, :], T.ones[:, :], [[-16, 8], [0, 64]], Alu.is_ge, 0.0, 0, 1), ["ones"], ["bu"])
    op("g", lambda: g.affine_select(T.bt[:, :], T.bu[:, :], [[16, 8], [0, 64]], Alu.is_ge, 0.0, 15, -1), ["bu"], ["bt"])
    iota(T.k1[:, :], [[1, E]], 1, 0, ["k1"], True)

    quant(T.uq[:, :], T.up[:, :], T.uin[:, :], ["uin"], ["uq"])
    quant(T.q0[:, 128:C], T.s0[:, 128:C], T.xin[:, 512:4 * C], ["xb"], ["qb0"])
    cp(T.ua[:, :].bitcast(dt.uint32), T.uq[:, :].bitcast(dt.uint32).indirect(T.uo[:, :]), ["uq", "uo"], ["ua"])
    act(T.uap[:, :], T.up[:, :].indirect(T.uo[:, :]), Act.Copy, ["uq", "uo"], ["uap"])
    fill(T.zero[:, :], 0.0, ["zero"])
    act(T.st16[:, :], T.st[:, :], Act.Identity, ["st"], ["st16"], bias=float(CENTER))
    for _ in repeat(T.rst, "rst", BL, NV * BL):
        pass
    for _ in zip(repeat(T.m4, "m4", 16, E), repeat(T.m16, "m16", 16, CW)):
        pass
    xs = tags("xA", 0, 4) + tags("xB", 0, 4)
    ka = [T.ka16]

    def late_constants():
        fill(T.et[:, :], 0.0, tags("et", 0, 4))
        for b in range(4):
            act(T.et[:, 512 * b + b:512 * b + 512:4], T.ident[:, :], Act.Copy, ["ident"], ["et%d" % b])
        act(T.x32[:, :], T.xin[:, :], Act.Copy, ["xa", "xb"], xs, scale=32.0)
        act(T.vh[:, 0:4 * C], T.xin[:, :], Act.Copy, ["xa", "xb"], ["vhx"], scale=0.5)
        for k in (1, 2, 3):
            lo = min(16 * SETS[k][0], CW - 128)
            quant(T["tq%d" % k][:, lo:CW], T["tp%d" % k][:, lo:CW], T.zero[:, 0:4 * (CW - lo)], ["zero"], ["tq%d" % k])
        quant(T.bq[:, :], T.bp[:, :], T.bt[:, :], ["bt"], ["bq"])
        fill(T.xt[:, 4 * H:512], 0.0, tags("xtB", 0, 4))
        fill(T.kd[:, 0:1], 0.0, ["kd0"])
        fill(T.ext[:, CW:E], 0.0, ["extz"])
        for pc, pt, mine in ((T.pc0, "pca", LATE[0]), (T.pc1, "pcb", LATE[1])):
            val = []
            for c in range(NC):
                lo, hi, n = SETS[max(0, c // 4 - 1)]
                val.append((0 if c < NV or c in mine else n) + E - n + 16 * len([k for k in mine if k >= hi]))
            c = 0
            while c < NC:
                e = c
                while e < NC and val[e] == val[c]:
                    e += 1
                fill(pc[:, c:e], float(val[c]), ["%s%d" % (pt, c)])
                c = e
        for pc, pt in ((T.pc0, "pca"), (T.pc1, "pcb")):
            ts(pc[:, 0:CW // 16], pc[:, 0:CW // 16], T.pf[:, 4:5], None, Alu.add, r=tags(pt, 0, NC) + ["pf4"], w=[pt])

    def scores(t, lo, hi):
        q, s = T["q%d" % t], T["s%d" % t]
        r = ["ua", "uap", "qa%d" % t, "qb%d" % t] + (["halo%d" % t] if hi > C else [])
        bank = 4 if lo == 0 else 6
        mm(bank, hi - lo, T.ua[:, 0:128], T.uap[:, 0:128], q[:, lo:hi], s[:, lo:hi], r)
        if t == 0:
            mm(bank + 1, hi - lo, T.ua[:, 128:256], T.uap[:, 128:256], q[:, lo:hi], s[:, lo:hi], r)

    def unpack(t):
        q, s = T["q%d" % t], T["s%d" % t]
        for b in range(4):
            mm(b, 128, T.eq[:, 128 * b:128 * b + 128], T.ep[:, 128 * b:128 * b + 128], q[:, E - 128:E], s[:, E - 128:E],
               ["eq", "qb%d" % t, "halo%d" % t])

    def halo_numbers():
        for b in range(4):
            act(T.vh[:, 4 * C + b:4 * E:4], T["ps%d" % b][:, 128 - H:128], Act.Copy, (), ["ps%d" % b, "vhd%d" % b], scale=0.5)

    def keys(t, at, lo, hi, klo, khi):
        d, u = 2 ** t, UNIT[t]
        w, wm, k, sc = [(T.w16, T.wm16, T.k16, T.ksc16), (T.w16, T.wmf, T.kf, T.ksc), (T.wf, T.wmf, T.kf, T.ksc)][t]
        st, cc = (T.st, T.cc) if t else (T.st16, T.cc0)
        kt = ("k16_" if t == 0 else "kf_") + str(klo)
        p0, p1 = ("ps4", "ps5") if lo == 0 else ("ps6", "ps7")
        if t == 0:
            ts(T.sa[:, lo:hi], T[p0][:, lo - at:hi - at], 0.0, 2 * u, Alu.is_gt, Alu.mult, w=[p0, "sa"])
            ts(T.sb[:, lo:hi], T[p1][:, lo - at:hi - at], 0.0, u, Alu.is_gt, Alu.mult, w=[p1, "sb"])
            tt(w[:, lo:hi], T.sa[:, lo:hi], T.sb[:, lo:hi], Alu.add, ["sa", "sb"], ["w"])
        else:
            ts(T.sa[:, lo:hi], T[p0][:, lo - at:hi - at], 0.0, u, Alu.is_gt, Alu.mult, w=[p0, "sa"])
            prev, pt = (T.k16, ["k16_0", "k16_%d" % PRE, "k16_e"]) if t == 1 else (T.pp, ["pp"])
            tt(w[:, lo:hi], T.sa[:, lo:hi], prev[:, lo:hi], Alu.add, ["sa"] + pt, ["w"])
        top = min(khi, E - d)
        ts(wm[:, klo:top], w[:, klo:top], MULT[t], 2 * u, Alu.mult, Alu.add, r=["w"], w=["wm"])
        ke = []
        if top < khi:
            ke = ["k16_e" if t == 0 else "kf_e"]
            ts(k[:, top:khi], w[:, top:khi], MULT[t], u, Alu.mult, Alu.add, r=["w"], w=ke)
        tt(k[:, klo:top], wm[:, klo:top], w[:, klo + d:top + d], Alu.add, ["wm", "w"], [kt])
        scan(sc[:, klo:khi], T.mk[:, klo:khi], k[:, klo:khi], 0.0, Alu.mult, Alu.max, ["mk", kt] + ke, ["sc"])
        tt(ka[0][:, klo:khi], k[:, klo:khi], st[:, klo:khi], Alu.add, [kt, "st", "st16"] + ke, ["ka%d" % klo])
        a, b = klo // 16, khi // 16
        ts(T.thx[:, a:b], sc[:, klo + 15:khi:16], T.pf[:, 0:1], None, Alu.mult, r=["sc", "pf0"], w=["thx"])
        tt(T.th[:, a:b], T.thx[:, a:b], cc[:, a:b], Alu.add, ["thx", "cc", "cc0"], ["th%d" % klo])

    def rows(c, e):
        k = max(0, c // 4 - 1)
        n = SETS[k][2]
        r = ["ka0", "th0"] + (["ka%d" % PRE, "th%d" % PRE] if n > PRE else [])
        out = T["tl%d" % k][:, c % 4:4 * n:4] if k else T.bits[:, c * BL + 2:(c + 1) * BL]
        if e == "a":
            act(out, ka[0][:, 0:n], Act.Sign, r, ["tl%d" % c, "acc%d" % c], bias=T.th[:, c:c + 1], scale=-1.0, accum_out=T.acc[:, c:c + 1])
        else:
            ts(out, ka[0][:, 0:n], T.th[:, c:c + 1], 2.0, Alu.is_lt, Alu.mult, r=r, w=["tl%d" % c])

    def first_set():
        for c in range(NV):
            rows(c, "v")
        scan(T.cnt[:, :], T.bits[:, :], T.rst[:, :], 0.0, Alu.add, Alu.min, tags("tl", 0, NV) + ["rst", "bz0", "bz1"], ["cnt"])

    def first_counts():
        cp(T.acc[:, 0:NV], T.cnt[:, BL - 1:NV * BL:BL], ["cnt"], tags("acc", 0, NV))

    def columns(k, start, stop):
        lo, hi, n = SETS[k]
        q, s = T["tq%d" % k], T["tp%d" % k]
        quant(q[:, 0:16 * lo], s[:, 0:16 * lo], T["tl%d" % k][:, 0:64 * lo], tags("tl", lo, hi), ["tq%d" % k])
        op("p", lambda: P.matmul_mx(T.ps5[:, 0:CW], T.bq[:, :], T.bp[:, :], q[:, :], s[:, :], start, stop), ["bq", "tq%d" % k], ["ps5"])

    xts = tags("xtA", 0, 4) + tags("xtB", 0, 4)
    for t in range(R):
        last = t == R - 1
        qn, sn = T["q%d" % (t + 1)], T["s%d" % (t + 1)]
        ka[0] = T.ka if t else T.ka16
        mine = LATE[min(t, 1)]
        scores(t, 0, C)
        if t > 0:
            act(T.vh[:, 0:4 * C], T.x32[:, :], Act.Copy, xs, ["vhx"], scale=1.0 / 64)
        keys(t, 0, 0, C, 0, PRE)
        for c in range(NV, NP):
            rows(c, "a")
        if t == 0:
            first_set()
            late_constants()
            first_counts()
            columns(1, True, False)
            columns(2, False, False)
            quant(T.vq[:, :], T.vp[:, :], T.vin[:, :], ["vin"], ["vq"])
            quant(T.eq[:, :], T.ep[:, :], T.et[:, :], tags("et", 0, 4), ["eq"])
        scores(t, E - 128, E)
        unpack(t)
        keys(t, E - 128, C, E, PRE, E)
        for c in list(range(20, NC)) + list(range(NP, 20)):
            if c not in mine:
                rows(c, "a")
        halo_numbers()
        for c in mine:
            rows(c, "v")
        if t > 0:
            first_set()
        else:
            columns(3, False, False)
        for j, c in enumerate(mine):
            b = T.tl3[:, c % 4:4 * CW:4]
            scan(T.cnu[:, j * CW:(j + 1) * CW], b, b, 0.0, Alu.add, Alu.max, ["tl%d" % c], ["cnu%d" % j])
        if t > 0:
            columns(1, True, False)
            columns(2, False, False)
            first_counts()
        columns(4, False, t == 0)
        cp(T.acc[:, mine[0]:mine[-1] + 1], T.cnu[:, CW - 1:len(mine) * CW:CW], tags("cnu", 0, len(mine)), tags("acc", mine[0], mine[-1] + 1))
        if t > 0:
            columns(3, False, True)
        tt(T.acc1[:, :], T.acc[:, :], (T.pc1 if t else T.pc0)[:, :], Alu.add, tags("acc", 0, NC) + ["pca", "pcb"], ["acc1"])
        scan(T.ext[:, 0:CW], T.m16[:, :], T.ps5[:, 0:CW], 0.0, Alu.add, Alu.max, ["m16"], ["ps5", "ext"])
        tt(T.acc2[:, :], T.acc1[:, :], T.ext[:, 15:E:16], Alu.subtract, ["acc1", "ext", "extz"], ["acc2"])
        ts(T.pos[:, :], T.acc2[:, :], 0.5, None, Alu.mult, r=["acc2"], w=["pos"])
        ps = ["pos"]
        ts(T.nmo[:, 0:18], T.acc2[:, 0:18], 0.5, -1.0, Alu.mult, Alu.add, r=["acc2"], w=["no"])
        cp(T.ordw[:, :].indirect(T.pos[:, :]), T.k1[:, :], ps + ["k1"], ["ordw"])
        ts(T.nmo[:, 18:36], T.pos[:, 0:18], 1.0, float(E - 1), Alu.add, Alu.min, r=ps, w=["mo"])
        h = H // 16
        vt = ["vhx"] + tags("vhd", 0, 4)

        def offsets(lo, hi, tag):
            scan(T.nms[:, lo:hi], T.m4[:, 0:hi - lo], T.nm[:, lo:hi], 0.0, Alu.add, Alu.max, ["m4", "n" + tag, "m" + tag], ["nms" + tag])
            ts(T.off[:, lo // 4:hi // 4], T.nms[:, lo + 3:hi:4], 4.0, T.pf[:, 3:4], Alu.mult, Alu.add, r=["nms" + tag, "pf3"], w=["off" + tag])

        def before_n(lo, hi, o, tag):
            act(T.gn[:, 4 * lo:4 * hi], T.vh[:, :].indirect(T.off[:, o:o + (hi - lo) // 4]), Act.Copy, vt + ["off" + tag], ["gn" + tag])

        def blend(lo, hi, o, z, zq, zp, n, bank, tag):
            tt(T.gm[:, 4 * lo:4 * hi], T.vh[:, :].indirect(T.off[:, o:o + (hi - lo) // 4]), T.gn[:, 4 * lo:4 * hi], Alu.max,
               vt + ["off" + tag, "gn" + tag], ["gm" + tag])
            tt(z[:, 0:4 * (hi - lo)], T.gm[:, 4 * lo:4 * hi], T.vh[:, 4 * lo:4 * hi], Alu.add, ["gm" + tag, "vhx"], ["z" + tag])
            quant(zq[:, :], zp[:, :], z[:, :], ["z" + tag, "zapad"], ["zq" + tag])
            for b in range(4):
                mm(bank + b, n, T.wq[:, 128 * b:128 * b + 128], T.wp[:, 128 * b:128 * b + 128], zq[:, :], zp[:, :], ["W", "zq" + tag])

        def state(lo, hi, bank, tag, scalar):
            for b in range(4):
                x = T.x32[:, 4 * lo + b:4 * hi:4]
                tt(x, T["ps%d" % (bank + b)][:, 0:hi - lo], x, Alu.add, (), ["ps%d" % (bank + b), "x%s%d" % (tag, b)])
                if scalar:
                    act(T.xt[:, 4 * lo + b:4 * hi:4], x, Act.Copy, ["x%s%d" % (tag, b)], ["xt%s%d" % (tag, b)], scale=1.0 / 32)
            if not scalar:
                ts(T.xt[:, 4 * lo:4 * hi], T.x32[:, 4 * lo:4 * hi], 1.0 / 32, None, Alu.mult, r=tags("x" + tag, 0, 4), w=tags("xt" + tag, 0, 4))

        act(T.nm[:, 0:H], T.ordw[:, :].indirect(T.nmo[:, 0:h]), Act.Copy, ["ordw", "no"], ["nA"])
        cp(T.nm[:, H:2 * H], T.ordw[:, :].indirect(T.nmo[:, 18:18 + h]), ["ordw", "mo"], ["mA"])
        act(T.nm[:, 2 * H:H + C], T.ordw[:, :].indirect(T.nmo[:, h:18]), Act.Copy, ["ordw", "no"], ["nB"])
        offsets(0, 2 * H, "A")
        before_n(0, H, 0, "A")
        cp(T.nm[:, H + C:2 * C], T.ordw[:, :].indirect(T.nmo[:, 18 + h:36]), ["ordw", "mo"], ["mB"])
        offsets(2 * H, 2 * C, "B")
        before_n(H, C, 2 * H // 4, "B")
        blend(0, H, H // 4, T.za, T.zqa, T.zpa, 128, 0, "A")
        if t > 0:
            scan(T.osc0[:, :], T.mk[:, :], T.ordw[:, :], 0.0, Alu.mult, Alu.max, ["mk", "ordw"], ["osc0"])
        state(0, H, 0, "A", last)
        if not last:
            quant(qn[:, 0:128], sn[:, 0:128], T.xt[:, 0:512], xts, ["qa%d" % (t + 1)])
            send(t + 1)
        if t > 0:
            ts(T.oo[:, :], T.osc0[:, 15:E:16], T.pf[:, 0:1], -1.0, Alu.mult, Alu.add, r=["osc0", "pf0"], w=["oo"])
            act(T.ks[:, :], T.kf[:, :].indirect(T.oo[:, :]), Act.Copy, ["kf_0", "kf_%d" % PRE, "kf_e", "oo"], ["ks"], scale=16.0)
        blend(H, C, (H + C) // 4, T.zb, T.zqb, T.zpb, C - H, 4, "B")
        if t > 0:
            tt(T.kd[:, 1:E], T.ks[:, 1:E], T.ks[:, 0:E - 1], Alu.subtract, ["ks"], ["kd"])
        state(H, C, 4, "B", t > 0)
        if t > 0:
            scan(T.lvs[:, :], T.kd[:, :], T.k1[:, :], 1.0, Alu.add, Alu.min, ["kd", "kd0", "k1"], ["lvs"])
            if last:
                act(T.pp[:, :], T.lvs[:, :].indirect(T.pos[:, :]), Act.Identity, ["lvs"] + ps, ["pp"], bias=-1.0)
                op("a", lambda: A.dma_start(T.lv[:, :], T.pp[0:128:16, :]), ["pp"], (), "out")
            else:
                act(T.pp[:, :], T.lvs[:, :].indirect(T.pos[:, :]), Act.Copy, ["lvs"] + ps, ["pp"], scale=2 * UNIT[t + 1])
        if not last:
            quant(qn[:, H:C], sn[:, H:C], T.xt[:, 4 * H:4 * C], tags("xtB", 0, 4) + ["qa%d" % (t + 1)], ["qb%d" % (t + 1)])

    quant(T.q3[:, 0:C], T.s3[:, 0:C], T.xt[:, :], xts, ["q3"])
    mm(0, C, T.vq[:, :], T.vp[:, :], T.q3[:, 0:C], T.s3[:, 0:C], ["vq", "q3"])
    op("s", lambda: g.sync.dma_start(T.oc[:, :], T.q3[:, 0:C].bitcast(dt.uint8)), ["q3"], (), "out")
    for k in range(4):
        op("s", lambda k=k: g.sync.dma_start(T.osc[4 * k:4 * k + 4, :], T.s3[32 * k:32 * k + 4, 0:C]), ["q3"], (), "out")
    cp(T.ysb[:, :], T.ps0[:, 0:C], (), ["ps0", "ysb"])
    op("s", lambda: g.sync.dma_start(T.y[:, :], T.ysb[:, :]), ["ysb"], (), "out")
    for s, v in total.items():
        if v:
            need("g", s, v)
